import numpy as np
import ml_dtypes


def mxq(x, axis, fmt="e4m3"):
    dtype, down = {"e4m3": (ml_dtypes.float8_e4m3fn, 7), "e5m2": (ml_dtypes.float8_e5m2, 14)}[fmt]
    v = np.moveaxis(np.asarray(x, np.float32).astype(ml_dtypes.bfloat16).astype(np.float64), axis, -1)
    blocks = v.reshape(v.shape[:-1] + (-1, 32))
    amax = np.abs(blocks).max(-1, keepdims=True)
    byte = np.maximum(np.where(amax > 0, np.frexp(amax)[1] - 1 + 127, 0) - down, 1)
    scale = np.exp2(byte - 127.0)
    codes = (blocks / scale).astype(np.float32).astype(dtype).astype(np.float64)
    return np.moveaxis((codes * scale).reshape(v.shape), -1, axis)


WIDE = False


def mx_kscale(k):
    if not WIDE:
        return np.ones(k)
    levels = np.array([10, -10, 5, -5, 0])
    if k % 512:
        return np.exp2(np.random.permutation(np.resize(levels, k // 32))).repeat(32)
    a = np.empty((k // 512, 16))
    for p in range(k // 512):
        a[p, :8] = np.random.permutation(np.resize(levels, 8))
        for g in range(8):
            far = levels[np.abs(levels - a[p, g]) >= 10]
            a[p, g + 8] = far[np.random.randint(len(far))]
    return np.exp2(a.ravel()).repeat(32)


def f64(x):
    return np.asarray(x).astype(np.float64)


def striped(idx):
    return np.tile(idx.reshape(-1, 16).T, (8, 1)).astype(np.uint16)


def unstriped(offs):
    return offs[:16].T.reshape(-1).astype(np.int64)


def striped8(idx):
    return np.concatenate([x.reshape(-1, 16).T for x in idx]).astype(np.uint16)


def runs(offs, k):
    lists = np.stack([offs[16 * r : 16 * r + 16].T.reshape(-1) for r in range(8)]).astype(np.int64)
    return lists[np.arange(k) % 512 // 64]


def pack_weight(w):
    k, n = w.shape
    w = f64(np.asarray(w, np.float32).astype(ml_dtypes.bfloat16)).reshape(k // 32, 32, n)
    amax = np.abs(w).max(1)
    byte = np.clip(np.where(amax > 0, np.frexp(amax)[1] - 1 + 127 - 7, 1), 1, 254)
    scaled = (w * np.exp2(127.0 - byte)[:, None, :]).reshape(k, n).astype(np.float32)
    words = np.ascontiguousarray(scaled.reshape(k // 512, 128, 4, n).transpose(0, 1, 3, 2)).astype(ml_dtypes.float8_e4m3fn).view(np.uint8)
    return words, np.ascontiguousarray(byte.astype(np.uint8).reshape(k // 512, 16, n))


def unpack_weight(words, scales):
    g, p, n, _ = words.shape
    vals = np.ascontiguousarray(words).view(ml_dtypes.float8_e4m3fn).astype(np.float64) * np.repeat(np.exp2(scales.astype(np.float64) - 127.0), 8, axis=1)[..., None]
    return vals.transpose(0, 1, 3, 2).reshape(g * 512, n)


def sigmoid(v):
    return 1.0 / (1.0 + np.exp(-np.maximum(v, -700.0)))


K, T, S, H, W = 512, 2048, 512, 512, 256


def setup_inputs():
    n = np.random.standard_normal
    s = mx_kscale(K)[:, None]
    u = mx_kscale(H)
    packed_xT = pack_weight(n((K, T)) * s)
    perm = np.stack([np.random.permutation(S) for _ in range(8)])
    return {
        "x_words": packed_xT[0],
        "x_scales": packed_xT[1],
        "w1": (n((K, H)) / np.sqrt(K) / s).astype(np.float32),
        "gn": (np.random.uniform(0.5, 1.5, (H, 1)) * u[:, None]).astype(np.float32),
        "w2": (n((H, H)) / np.sqrt(H) / u[:, None]).astype(np.float32),
        "offs": striped(np.random.permutation(T)[:S]),
        "n1": striped8(np.stack([np.random.permutation(S) for _ in range(8)])),
        "n2": striped8(np.stack([np.random.permutation(S) for _ in range(8)])),
        "n3": striped8(perm[:, :W]),
        "n4": striped8(perm[:, W:]),
        "n5": striped8(np.stack([np.random.permutation(S) for _ in range(8)])),
        "n6": striped8(np.stack([np.random.permutation(S) for _ in range(8)])),
    }


def reference(x_words, x_scales, w1, gn, w2, offs, n1, n2, n3, n4, n5, n6):
    xq = unpack_weight(x_words, x_scales)[:, unstriped(offs)]
    y = mxq(f64(w1), 0, "e4m3").T @ xq
    z = f64(gn) * (0.75 * (y[np.arange(H)[:, None], runs(n1, H)] + y[np.arange(H)[:, None], runs(n2, H)]) - y)
    w2q = mxq(f64(w2), 0, "e4m3")
    a = w2q.T @ mxq(z, 0, "e4m3")
    pb = y[np.arange(H)[:, None], runs(n4, H)]
    pa = y[np.arange(H)[:, None], runs(n3, H)]
    rb = pb * sigmoid(pb - pa)
    ra = pa * sigmoid(pa - pb)
    ds = np.zeros((H, S))
    ds[np.arange(H)[:, None], runs(n3, H)] = ra
    dt = ds.copy()
    dt[np.arange(H)[:, None], runs(n4, H)] = rb
    z2 = f64(gn) * dt
    b = w2q.T @ mxq(z2, 0, "e4m3")
    return (a - (a[np.arange(H)[:, None], runs(n5, H)])) / (np.abs(b) + np.abs(b[np.arange(H)[:, None], runs(n6, H)]) + 0.5)

@@ -1,0 +1,249 @@
+from contextlib import ExitStack
+
+import concourse.mybir as mybir
+from concourse.masks import make_identity
+
+K, T, S, H, W = 512, 2048, 512, 512, 256
+FLOPS = 3 * 2 * 512 * 512 * 512
+
+F32 = mybir.dt.float32
+BF16 = mybir.dt.bfloat16
+I32 = mybir.dt.int32
+U32 = mybir.dt.uint32
+U16 = mybir.dt.uint16
+U8 = mybir.dt.uint8
+FP8X4 = mybir.dt.float8_e4m3fn_x4
+ALU = mybir.AluOpType
+ACT = mybir.ActivationFunctionType
+
+P = 128
+PACK = 4
+
+
+def tile_picked_tienormblapduel_none_p_kernel(
+    tc, x_words, x_scales, w1, gn, w2, offs, n1, n2, n3, n4, n5, n6, out
+):
+    nc = tc.nc
+    with ExitStack() as ctx:
+        lists = ctx.enter_context(tc.tile_pool(name="lists", bufs=1))
+        keep = ctx.enter_context(tc.tile_pool(name="keep", bufs=1))
+        psum = ctx.enter_context(tc.psum_pool(name="psum", bufs=1))
+
+        def load_list(ap, name):
+            tile = lists.tile(list(ap.shape), U16, name=name)
+            nc.sync.dma_start(tile[:], ap)
+            return tile
+
+        def sb(shape, dtype, name):
+            return keep.tile(shape, dtype, name=name, align_bytes=64)
+
+        def bank(tag, name):
+            return psum.tile([P, 512], F32, name=name, tag=tag)
+
+        xs = sb([P, T], U8, "xs")
+        nc.vector.memset(xs[:].bitcast(I32), 0)
+        offs_t = load_list(offs, "offs_t")
+        w1_raw = [sb([P, PACK, 256], F32, f"w1_raw{h}") for h in range(2)]
+        w1_v = w1.rearrange("(p j) c -> p j c", j=PACK)
+        nc.sync.dma_start(w1_raw[0][:], w1_v[:, :, :256])
+        for q in range(4):
+            nc.sync.dma_start(xs[32 * q : 32 * q + 4, :].bitcast(I32), x_scales[0, 4 * q : 4 * q + 4, :].bitcast(I32))
+        nc.sync.dma_start(w1_raw[1][:], w1_v[:, :, 256:])
+        xw = sb([P, T], I32, "xw")
+        nc.sync.dma_start(xw[:], x_words[0].rearrange("p n t -> p (n t)").bitcast(I32))
+        gain = sb([P, PACK], F32, "gain")
+        nc.sync.dma_start(gain[:], gn.rearrange("(p t) o -> p (t o)", t=PACK))
+        n3_t = load_list(n3, "n3_t")
+        n4_t = load_list(n4, "n4_t")
+        n1_t = load_list(n1, "n1_t")
+        n2_t = load_list(n2, "n2_t")
+        n6_t = load_list(n6, "n6_t")
+        n5_t = load_list(n5, "n5_t")
+        w2_raw = sb([P, PACK, H], F32, "w2_raw")
+        nc.sync.dma_start(w2_raw[:], w2.rearrange("(p j) c -> p j c", j=PACK))
+
+        zero = sb([P, 1], F32, "zero")
+        nc.vector.memset(zero[:], 0.0)
+        half = sb([P, 1], F32, "half")
+        nc.scalar.activation(half[:], zero[:], ACT.Sigmoid)
+
+        ident = sb([P, P], F32, "ident")
+        make_identity(nc, ident[:])
+
+        win = [sb([P, 2 * S], F32, f"win{t}") for t in range(PACK)]
+        aux = [sb([P, 2 * S], F32, f"aux{t}") for t in range(PACK)]
+        for t in range(PACK):
+            nc.vector.memset(win[t][:, S:], 0.0)
+
+        sg = sb([P, S], U8, "sg")
+        nc.vector.tensor_copy(sg[:], xs[:].indirect(offs_t[:]))
+        w1_bf = sb([P, PACK * H], BF16, "w1_bf")
+        w1_bv = w1_bf[:].rearrange("p (t m j) -> p m t j", t=PACK, j=PACK)
+        for h in range(2):
+            nc.vector.tensor_copy(w1_bv[:, 64 * h : 64 * (h + 1)], w1_raw[h][:].rearrange("p j (m t) -> p m t j", t=PACK))
+        w1_c = sb([P, H], U32, "w1_c")
+        w1_s = sb([P, H], U8, "w1_s")
+        nc.vector.quantize_mx(w1_c[:].bitcast(FP8X4), w1_s[:], w1_bf[:])
+        xg = sb([P, S], U32, "xg")
+        nc.vector.tensor_copy(xg[:], xw[:].bitcast(U32).indirect(offs_t[:]))
+
+        safe = sb([P, PACK], F32, "safe")
+        inv = sb([P, PACK], F32, "inv")
+        ninv = sb([P, PACK], F32, "ninv")
+        cgain = sb([P, PACK], F32, "cgain")
+        nc.vector.scalar_tensor_tensor(safe[:], gain[:], 0.0, gain[:], ALU.is_equal, ALU.add)
+        nc.vector.tensor_scalar(cgain[:], gain[:], -4.0 / 3.0, None, ALU.mult)
+        nc.vector.reciprocal(inv[:], safe[:])
+        nc.vector.tensor_scalar(ninv[:], inv[:], -1.0, None, ALU.mult)
+
+        def product(w_c, w_s, r_c, r_s, name):
+            banks = []
+            for t in range(PACK):
+                acc = bank(f"mm{t}", f"{name}{t}")
+                cols = slice(P * t, P * (t + 1))
+                nc.tensor.matmul_mx(acc[:], lhsT=w_c[:, cols].bitcast(FP8X4), lhsT_scale=w_s[:, cols],
+                                    rhs=r_c[:].bitcast(FP8X4), rhs_scale=r_s[:], start=True, stop=True)
+                banks.append(acc)
+            return banks
+
+        y = product(w1_c, w1_s, xg, sg, "y")
+        for t in range(PACK):
+            nc.scalar.activation(win[t][:, :S], y[t][:], ACT.Copy, scale=gain[:, t : t + 1])
+
+        pa = [sb([P, W], F32, f"pa{t}") for t in range(PACK)]
+        pb = [sb([P, W], F32, f"pb{t}") for t in range(PACK)]
+        df = [sb([P, W], F32, f"df{t}") for t in range(PACK)]
+        sa = [sb([P, W], F32, f"sa{t}") for t in range(PACK)]
+        sbb = [sb([P, W], F32, f"sbb{t}") for t in range(PACK)]
+        dt = [sb([P, S], F32, f"dt{t}") for t in range(PACK)]
+
+        def duel_fetch(t):
+            nc.vector.tensor_copy(pa[t][:], win[t][:].indirect(n3_t[:]))
+            nc.vector.tensor_copy(pb[t][:], win[t][:].indirect(n4_t[:]))
+
+        def duel_gate(t):
+            nc.vector.tensor_tensor(df[t][:], pb[t][:], pa[t][:], ALU.subtract)
+            nc.scalar.activation(sa[t][:], df[t][:], ACT.Sigmoid, scale=ninv[:, t : t + 1])
+            nc.scalar.activation(sbb[t][:], df[t][:], ACT.Sigmoid, scale=inv[:, t : t + 1])
+
+        def put_a(t):
+            nc.vector.tensor_tensor(dt[t][:].indirect(n3_t[:]), pa[t][:], sa[t][:], ALU.mult)
+
+        def put_b(t):
+            nc.vector.tensor_tensor(dt[t][:].indirect(n4_t[:]), pb[t][:], sbb[t][:], ALU.mult)
+
+        def add_transposed(dst, terms):
+            for i, term in enumerate(terms):
+                nc.tensor.matmul(dst, lhsT=term, rhs=ident[:], is_transpose=True, start=(i == 0), stop=(i == len(terms) - 1))
+
+        def turn_pair(u, terms_of, scale, name):
+            res = []
+            for h in range(2):
+                tr = bank(f"tr{h}", f"{name}tr{u}{h}")
+                trv = tr[:].rearrange("p (b e m) -> p b e m", b=2, e=2)
+                for e in range(2):
+                    for b in range(2):
+                        blk = 2 * h + b
+                        add_transposed(trv[:, b, e, :], [x[:, P * blk : P * (blk + 1)] for x in terms_of(2 * u + e)])
+                zt = sb([P, 512], BF16, f"{name}zt{u}{h}")
+                nc.scalar.activation(zt[:].rearrange("p (b m e) -> p b m e", b=2, e=2),
+                                     tr[:].rearrange("p (b e m) -> p b m e", b=2, e=2), ACT.Copy, scale=scale)
+                res.append(zt)
+            return res
+
+        def back_pair(u, zts, bks):
+            for h in range(2):
+                words = zts[h][:].bitcast(F32)
+                for b in range(2):
+                    nc.tensor.transpose(bks[h][:, 256 * u + P * b : 256 * u + P * (b + 1)], words[:, P * b : P * (b + 1)], ident[:])
+
+        def finish(bks, name):
+            zq = sb([P, PACK * S], BF16, f"{name}q")
+            zw = zq[:].bitcast(F32).rearrange("p (j u) -> p j u", u=2)
+            for h in range(2):
+                nc.scalar.copy(zw[:, 256 * h : 256 * (h + 1), :], bks[h][:].rearrange("p (u j) -> p j u", u=2))
+            codes = sb([P, S], U32, f"{name}c")
+            scales = sb([P, S], U8, f"{name}s")
+            nc.vector.quantize_mx(codes[:].bitcast(FP8X4), scales[:], zq[:])
+            return codes, scales
+
+        duel_fetch(0)
+        duel_fetch(1)
+        duel_gate(0)
+        duel_gate(1)
+        duel_fetch(2)
+        duel_fetch(3)
+        duel_gate(2)
+        duel_gate(3)
+        bks2 = [bank(f"bk{h}", f"z2bk{h}") for h in range(2)]
+        for u in range(2):
+            put_a(2 * u)
+            put_a(2 * u + 1)
+            put_b(2 * u)
+            put_b(2 * u + 1)
+            zts = turn_pair(u, lambda t: [dt[t]], 1.0, "z2")
+            back_pair(u, zts, bks2)
+
+        for t in range(PACK):
+            nc.scalar.activation(aux[t][:, S:], y[t][:], ACT.Copy, scale=cgain[:, t : t + 1])
+        w2_bf = sb([P, PACK * H], BF16, "w2_bf")
+        w2_bv = w2_bf[:].rearrange("p (t m j) -> p m t j", t=PACK, j=PACK)
+        w2_rv = w2_raw[:].rearrange("p j (m t) -> p m t j", t=PACK)
+        for h in range(4):
+            nc.scalar.copy(w2_bv[:, 32 * h : 32 * (h + 1)], w2_rv[:, 32 * h : 32 * (h + 1)])
+        w2_c = sb([P, H], U32, "w2_c")
+        w2_s = sb([P, H], U8, "w2_s")
+        nc.vector.quantize_mx(w2_c[:].bitcast(FP8X4), w2_s[:], w2_bf[:])
+
+        z2_c, z2_s = finish(bks2, "z2")
+        b = product(w2_c, w2_s, z2_c, z2_s, "b")
+        for t in range(PACK):
+            nc.scalar.activation(aux[t][:, :S], b[t][:], ACT.Abs)
+
+        g1 = [sb([P, S], F32, f"g1{t}") for t in range(PACK)]
+        g2 = [sb([P, S], F32, f"g2{t}") for t in range(PACK)]
+        bks1 = [bank(f"bk{h}", f"zbk{h}") for h in range(2)]
+        for u in range(2):
+            for t in (2 * u, 2 * u + 1):
+                nc.vector.tensor_copy(g1[t][:], win[t][:].indirect(n1_t[:]))
+                nc.vector.tensor_copy(g2[t][:], win[t][:].indirect(n2_t[:]))
+            zts = turn_pair(u, lambda t: [aux[t][:, S:], g1[t], g2[t]], 0.75, "z")
+            back_pair(u, zts, bks1)
+        z_c, z_s = finish(bks1, "z")
+        a = product(w2_c, w2_s, z_c, z_s, "a")
+        for t in range(PACK):
+            nc.scalar.copy(win[t][:, :S], a[t][:])
+
+        g6 = [sb([P, S], F32, f"g6{t}") for t in range(PACK)]
+        rec = []
+        for t in range(PACK):
+            nc.vector.tensor_copy(g6[t][:], aux[t][:].indirect(n6_t[:]))
+        for t in range(PACK):
+            tr = bank(f"tr{t % 2}", f"den{t}")
+            for blk in range(4):
+                cols = slice(P * blk, P * (blk + 1))
+                add_transposed(tr[:, cols], [aux[t][:, cols], g6[t][:, cols]])
+            rs = sb([P, S], F32, f"rs{t}")
+            nc.scalar.activation(rs[:], tr[:], ACT.Abs_reciprocal_sqrt, bias=half[:])
+            rq = sb([P, S], F32, f"rq{t}")
+            nc.scalar.activation(rq[:], rs[:], ACT.Square)
+            rb = bank(f"mm{t}", f"rec{t}")
+            for blk in range(4):
+                cols = slice(P * blk, P * (blk + 1))
+                nc.tensor.transpose(rb[:, cols], rq[:, cols], ident[:])
+            rec.append(rb)
+
+        out_v = out.rearrange("(p t) c -> p t c", t=PACK)
+        g5 = [sb([P, S], F32, f"g5{t}") for t in range(PACK)]
+        num = [sb([P, S], F32, f"num{t}") for t in range(PACK)]
+        res = [sb([P, S], F32, f"res{t}") for t in range(PACK)]
+        for step in range(PACK + 2):
+            if step < PACK:
+                nc.vector.tensor_copy(g5[step][:], win[step][:].indirect(n5_t[:]))
+            if 1 <= step <= PACK:
+                t = step - 1
+                nc.vector.tensor_tensor(num[t][:], win[t][:, :S], g5[t][:], ALU.subtract)
+            if step >= 2:
+                t = step - 2
+                nc.vector.tensor_tensor(res[t][:], num[t][:], rec[t][:], ALU.mult)
+                nc.sync.dma_start(out_v[:, t, :], res[t][:])

@@ -43,6 +43,8 @@ def tile_picked_tienormblapduel_none_p_kernel(
         xs = sb([P, T], U8, "xs")
         nc.vector.memset(xs[:].bitcast(I32), 0)
         offs_t = load_list(offs, "offs_t")
+        gain = sb([P, PACK], F32, "gain")
+        nc.sync.dma_start(gain[:], gn.rearrange("(p t) o -> p (t o)", t=PACK))
         w1_raw = [sb([P, PACK, 256], F32, f"w1_raw{h}") for h in range(2)]
         w1_v = w1.rearrange("(p j) c -> p j c", j=PACK)
         nc.sync.dma_start(w1_raw[0][:], w1_v[:, :, :256])
@@ -51,8 +53,6 @@ def tile_picked_tienormblapduel_none_p_kernel(
         nc.sync.dma_start(w1_raw[1][:], w1_v[:, :, 256:])
         xw = sb([P, T], I32, "xw")
         nc.sync.dma_start(xw[:], x_words[0].rearrange("p n t -> p (n t)").bitcast(I32))
-        gain = sb([P, PACK], F32, "gain")
-        nc.sync.dma_start(gain[:], gn.rearrange("(p t) o -> p (t o)", t=PACK))
         n3_t = load_list(n3, "n3_t")
         n4_t = load_list(n4, "n4_t")
         n1_t = load_list(n1, "n1_t")
@@ -64,6 +64,8 @@ def tile_picked_tienormblapduel_none_p_kernel(
 
         zero = sb([P, 1], F32, "zero")
         nc.vector.memset(zero[:], 0.0)
+        four = sb([P, 1], F32, "four")
+        nc.vector.memset(four[:], 4.0)
         half = sb([P, 1], F32, "half")
         nc.scalar.activation(half[:], zero[:], ACT.Sigmoid)
 
@@ -75,6 +77,15 @@ def tile_picked_tienormblapduel_none_p_kernel(
         for t in range(PACK):
             nc.vector.memset(win[t][:, S:], 0.0)
 
+        safe = sb([P, PACK], F32, "safe")
+        inv = sb([P, PACK], F32, "inv")
+        ninv = sb([P, PACK], F32, "ninv")
+        cgain = sb([P, PACK], F32, "cgain")
+        nc.vector.scalar_tensor_tensor(safe[:], gain[:], 0.0, gain[:], ALU.is_equal, ALU.add)
+        nc.vector.tensor_scalar(cgain[:], gain[:], half[:], -8.0 / 3.0, ALU.mult, ALU.mult)
+        nc.vector.reciprocal(inv[:], safe[:])
+        nc.vector.tensor_scalar(ninv[:], inv[:], -1.0, None, ALU.mult)
+
         sg = sb([P, S], U8, "sg")
         nc.vector.tensor_copy(sg[:], xs[:].indirect(offs_t[:]))
         w1_bf = sb([P, PACK * H], BF16, "w1_bf")
@@ -85,16 +96,8 @@ def tile_picked_tienormblapduel_none_p_kernel(
         w1_s = sb([P, H], U8, "w1_s")
         nc.vector.quantize_mx(w1_c[:].bitcast(FP8X4), w1_s[:], w1_bf[:])
         xg = sb([P, S], U32, "xg")
-        nc.vector.tensor_copy(xg[:], xw[:].bitcast(U32).indirect(offs_t[:]))
-
-        safe = sb([P, PACK], F32, "safe")
-        inv = sb([P, PACK], F32, "inv")
-        ninv = sb([P, PACK], F32, "ninv")
-        cgain = sb([P, PACK], F32, "cgain")
-        nc.vector.scalar_tensor_tensor(safe[:], gain[:], 0.0, gain[:], ALU.is_equal, ALU.add)
-        nc.vector.tensor_scalar(cgain[:], gain[:], -4.0 / 3.0, None, ALU.mult)
-        nc.vector.reciprocal(inv[:], safe[:])
-        nc.vector.tensor_scalar(ninv[:], inv[:], -1.0, None, ALU.mult)
+        for h in range(2):
+            nc.vector.tensor_copy(xg[:, W * h : W * (h + 1)], xw[:].bitcast(U32).indirect(offs_t[:, 16 * h : 16 * (h + 1)]))
 
         def product(w_c, w_s, r_c, r_s, name):
             banks = []
@@ -106,48 +109,66 @@ def tile_picked_tienormblapduel_none_p_kernel(
                 banks.append(acc)
             return banks
 
-        y = product(w1_c, w1_s, xg, sg, "y")
-        for t in range(PACK):
-            nc.scalar.activation(win[t][:, :S], y[t][:], ACT.Copy, scale=gain[:, t : t + 1])
+        pieces = []
+        for tag, t, c0, c1 in [("tr0", 0, 0, W), ("mm0", 0, W, S)] + [(f"mm{t}", t, 0, S) for t in range(1, PACK)]:
+            acc = bank(tag, f"y{t}{c0}")[:, : c1 - c0]
+            cols = slice(P * t, P * (t + 1))
+            nc.tensor.matmul_mx(acc, lhsT=w1_c[:, cols].bitcast(FP8X4), lhsT_scale=w1_s[:, cols],
+                                rhs=xg[:, c0:c1].bitcast(FP8X4), rhs_scale=sg[:, c0:c1], start=True, stop=True)
+            pieces.append((acc, t, c0, c1))
+        for i, (acc, t, c0, c1) in enumerate(pieces):
+            if i == 1:
+                nc.vector.tensor_scalar(win[t][:, c0:c1], acc, gain[:, t : t + 1], None, ALU.mult)
+            else:
+                nc.scalar.activation(win[t][:, c0:c1], acc, ACT.Copy, scale=gain[:, t : t + 1])
 
-        pa = [sb([P, W], F32, f"pa{t}") for t in range(PACK)]
-        pb = [sb([P, W], F32, f"pb{t}") for t in range(PACK)]
-        df = [sb([P, W], F32, f"df{t}") for t in range(PACK)]
-        sa = [sb([P, W], F32, f"sa{t}") for t in range(PACK)]
-        sbb = [sb([P, W], F32, f"sbb{t}") for t in range(PACK)]
+        pab2 = [sb([P, 2 * S], F32, f"pab{u}") for u in range(2)]
+        pab = [pab2[t // 2][:, S * (t % 2) : S * (t % 2 + 1)] for t in range(PACK)]
+        sab = [sb([P, S], F32, f"sab{t}")[:] for t in range(PACK)]
+        pa = [x[:, :W] for x in pab]
+        pb = [x[:, W:] for x in pab]
+        sa = [x[:, :W] for x in sab]
+        sbb = [x[:, W:] for x in sab]
+        df = [sb([P, 2 * W], F32, f"df{u}") for u in range(2)]
         dt = [sb([P, S], F32, f"dt{t}") for t in range(PACK)]
 
         def duel_fetch(t):
-            nc.vector.tensor_copy(pa[t][:], win[t][:].indirect(n3_t[:]))
-            nc.vector.tensor_copy(pb[t][:], win[t][:].indirect(n4_t[:]))
+            nc.vector.tensor_copy(pa[t], win[t][:].indirect(n3_t[:]))
+            nc.vector.tensor_copy(pb[t], win[t][:].indirect(n4_t[:]))
 
-        def duel_gate(t):
-            nc.vector.tensor_tensor(df[t][:], pb[t][:], pa[t][:], ALU.subtract)
-            nc.scalar.activation(sa[t][:], df[t][:], ACT.Sigmoid, scale=ninv[:, t : t + 1])
-            nc.scalar.activation(sbb[t][:], df[t][:], ACT.Sigmoid, scale=inv[:, t : t + 1])
+        def duel_gate(u):
+            pv = pab2[u][:].rearrange("p (e s w) -> p e s w", e=2, s=2)
+            nc.vector.tensor_tensor(df[u][:].rearrange("p (e w) -> p e w", e=2), pv[:, :, 1, :], pv[:, :, 0, :], ALU.subtract)
+            for dst, scale in ((sa, ninv), (sbb, inv)):
+                for e in range(2):
+                    t = 2 * u + e
+                    nc.scalar.activation(dst[t], df[u][:, W * e : W * (e + 1)], ACT.Sigmoid, scale=scale[:, t : t + 1])
 
         def put_a(t):
-            nc.vector.tensor_tensor(dt[t][:].indirect(n3_t[:]), pa[t][:], sa[t][:], ALU.mult)
+            nc.vector.tensor_tensor(dt[t][:].indirect(n3_t[:]), pa[t], sa[t], ALU.mult)
 
         def put_b(t):
-            nc.vector.tensor_tensor(dt[t][:].indirect(n4_t[:]), pb[t][:], sbb[t][:], ALU.mult)
+            nc.vector.tensor_tensor(dt[t][:].indirect(n4_t[:]), pb[t], sbb[t], ALU.mult)
 
         def add_transposed(dst, terms):
             for i, term in enumerate(terms):
                 nc.tensor.matmul(dst, lhsT=term, rhs=ident[:], is_transpose=True, start=(i == 0), stop=(i == len(terms) - 1))
 
-        def turn_pair(u, terms_of, scale, name):
+        def turn_pair(u, terms_of, scale, name, tags):
+            trs = [bank(tags[h], f"{name}tr{u}{h}") for h in range(2)]
+            for e in range(2):
+                terms = terms_of(2 * u + e)
+                for b in range(2):
+                    for i, term in enumerate(terms):
+                        for h in range(2):
+                            blk = 2 * h + b
+                            nc.tensor.matmul(trs[h][:, 2 * P * b + P * e : 2 * P * b + P * (e + 1)], lhsT=term[:, P * blk : P * (blk + 1)],
+                                             rhs=ident[:], is_transpose=True, start=(i == 0), stop=(i == len(terms) - 1))
             res = []
             for h in range(2):
-                tr = bank(f"tr{h}", f"{name}tr{u}{h}")
-                trv = tr[:].rearrange("p (b e m) -> p b e m", b=2, e=2)
-                for e in range(2):
-                    for b in range(2):
-                        blk = 2 * h + b
-                        add_transposed(trv[:, b, e, :], [x[:, P * blk : P * (blk + 1)] for x in terms_of(2 * u + e)])
                 zt = sb([P, 512], BF16, f"{name}zt{u}{h}")
                 nc.scalar.activation(zt[:].rearrange("p (b m e) -> p b m e", b=2, e=2),
-                                     tr[:].rearrange("p (b e m) -> p b m e", b=2, e=2), ACT.Copy, scale=scale)
+                                     trs[h][:].rearrange("p (b e m) -> p b m e", b=2, e=2), ACT.Copy, scale=scale)
                 res.append(zt)
             return res
 
@@ -165,27 +186,26 @@ def tile_picked_tienormblapduel_none_p_kernel(
             codes = sb([P, S], U32, f"{name}c")
             scales = sb([P, S], U8, f"{name}s")
             nc.vector.quantize_mx(codes[:].bitcast(FP8X4), scales[:], zq[:])
-            return codes, scales
+            return codes, scales, zq[:].bitcast(F32)
 
         duel_fetch(0)
         duel_fetch(1)
         duel_gate(0)
-        duel_gate(1)
         duel_fetch(2)
         duel_fetch(3)
-        duel_gate(2)
-        duel_gate(3)
-        bks2 = [bank(f"bk{h}", f"z2bk{h}") for h in range(2)]
-        for u in range(2):
-            put_a(2 * u)
-            put_a(2 * u + 1)
-            put_b(2 * u)
-            put_b(2 * u + 1)
-            zts = turn_pair(u, lambda t: [dt[t]], 1.0, "z2")
-            back_pair(u, zts, bks2)
-
-        for t in range(PACK):
-            nc.scalar.activation(aux[t][:, S:], y[t][:], ACT.Copy, scale=cgain[:, t : t + 1])
+        duel_gate(1)
+        half2 = sb([P, 1], F32, "half2")
+        nc.scalar.activation(half2[:], sbb[3][:, 0:1], ACT.Abs_reciprocal_sqrt, bias=four[:], scale=0.0)
+        for acc, t, c0, c1 in pieces:
+            nc.scalar.activation(aux[t][:, S + c0 : S + c1], acc, ACT.Copy, scale=cgain[:, t : t + 1])
+        bks1 = [bank(f"mm{2 + h}", f"zbk{h}") for h in range(2)]
+        g1 = [sb([P, S], F32, "g10")[:], sb([P, S], F32, "g11")[:]]
+        g2 = [sb([P, S], F32, "g20")[:], sb([P, S], F32, "g21")[:]]
+        for t in range(2):
+            nc.vector.tensor_copy(g1[t], win[t][:].indirect(n1_t[:]))
+            nc.vector.tensor_copy(g2[t], win[t][:].indirect(n2_t[:]))
+        zts = turn_pair(0, lambda t: [aux[t][:, S:], g1[t], g2[t]], 0.75, "z", ("tr0", "tr1"))
+        back_pair(0, zts, bks1)
         w2_bf = sb([P, PACK * H], BF16, "w2_bf")
         w2_bv = w2_bf[:].rearrange("p (t m j) -> p m t j", t=PACK, j=PACK)
         w2_rv = w2_raw[:].rearrange("p j (m t) -> p m t j", t=PACK)
@@ -195,55 +215,112 @@ def tile_picked_tienormblapduel_none_p_kernel(
         w2_s = sb([P, H], U8, "w2_s")
         nc.vector.quantize_mx(w2_c[:].bitcast(FP8X4), w2_s[:], w2_bf[:])
 
-        z2_c, z2_s = finish(bks2, "z2")
-        b = product(w2_c, w2_s, z2_c, z2_s, "b")
-        for t in range(PACK):
-            nc.scalar.activation(aux[t][:, :S], b[t][:], ACT.Abs)
-
-        g1 = [sb([P, S], F32, f"g1{t}") for t in range(PACK)]
-        g2 = [sb([P, S], F32, f"g2{t}") for t in range(PACK)]
-        bks1 = [bank(f"bk{h}", f"zbk{h}") for h in range(2)]
+        bks2 = [bank(f"bk{h}", f"z2bk{h}") for h in range(2)]
         for u in range(2):
-            for t in (2 * u, 2 * u + 1):
-                nc.vector.tensor_copy(g1[t][:], win[t][:].indirect(n1_t[:]))
-                nc.vector.tensor_copy(g2[t][:], win[t][:].indirect(n2_t[:]))
-            zts = turn_pair(u, lambda t: [aux[t][:, S:], g1[t], g2[t]], 0.75, "z")
-            back_pair(u, zts, bks1)
-        z_c, z_s = finish(bks1, "z")
-        a = product(w2_c, w2_s, z_c, z_s, "a")
-        for t in range(PACK):
-            nc.scalar.copy(win[t][:, :S], a[t][:])
+            put_a(2 * u)
+            put_a(2 * u + 1)
+            put_b(2 * u)
+            put_b(2 * u + 1)
+            zts = turn_pair(u, lambda t: [dt[t]], 1.0, "z2", ("tr0", "tr1"))
+            back_pair(u, zts, bks2)
 
-        g6 = [sb([P, S], F32, f"g6{t}") for t in range(PACK)]
+        def mx(acc, w_c, w_s, t, r_c, r_s):
+            cols = slice(P * t, P * (t + 1))
+            nc.tensor.matmul_mx(acc, lhsT=w_c[:, cols].bitcast(FP8X4), lhsT_scale=w_s[:, cols],
+                                rhs=r_c.bitcast(FP8X4), rhs_scale=r_s, start=True, stop=True)
+
+        z2_c, z2_s, z2_w = finish(bks2, "z2")
+
+        def b_tile(t):
+            acc = bank(("mm0", "mm1", "tr0", "tr1")[t], f"b{t}")
+            mx(acc[:], w2_c, w2_s, t, z2_c[:], z2_s[:])
+            nc.scalar.activation(aux[t][:, :S], acc[:], ACT.Abs)
+
+        room = [[pab[3][:, :W], pab[3][:, W:], sab[3][:, :W], sab[3][:, W:]], [z2_w[:, W * i : W * (i + 1)] for i in range(4)]]
+        zq = [sb([P, 2 * S], BF16, f"zq{h}") for h in range(2)]
+        z_c = sb([P, S], U32, "zc")
+        z_s = sb([P, S], U8, "zs")
+
+        def z_half(h):
+            trs = [bank(f"bk{blk}", f"ztr{h}{blk}") for blk in range(2)]
+            for e in range(2):
+                t = 2 + e
+                f1, f2 = room[h][2 * e], room[h][2 * e + 1]
+                nc.vector.tensor_copy(f1, win[t][:].indirect(n1_t[:, 16 * h : 16 * (h + 1)]))
+                nc.vector.tensor_copy(f2, win[t][:].indirect(n2_t[:, 16 * h : 16 * (h + 1)]))
+                terms = [aux[t][:, S + W * h : S + W * (h + 1)], f1, f2]
+                for i in range(3):
+                    for blk in range(2):
+                        nc.tensor.matmul(trs[blk][:, P * e : P * (e + 1)], lhsT=terms[i][:, P * blk : P * (blk + 1)], rhs=ident[:],
+                                         is_transpose=True, start=(i == 0), stop=(i == 2))
+            for blk in range(2):
+                zt = sb([P, W], BF16, f"zt1{h}{blk}")
+                nc.scalar.activation(zt[:].rearrange("p (m e) -> p m e", e=2),
+                                     trs[blk][:, :W].rearrange("p (e m) -> p m e", e=2), ACT.Copy, scale=0.75)
+                nc.tensor.transpose(bks1[h][:, W + P * blk : W + P * (blk + 1)], zt[:].bitcast(F32), ident[:])
+            nc.scalar.copy(zq[h][:].bitcast(F32).rearrange("p (j u) -> p j u", u=2), bks1[h][:].rearrange("p (u j) -> p j u", u=2))
+            nc.vector.quantize_mx(z_c[:, W * h : W * (h + 1)].bitcast(FP8X4), z_s[:, W * h : W * (h + 1)], zq[h][:])
+
+        def a_part(t, c0, c1):
+            acc = bank(("mm0", "mm1", "tr0", "tr1")[t], f"a{t}{c0}")[:, : c1 - c0]
+            mx(acc, w2_c, w2_s, t, z_c[:, c0:c1], z_s[:, c0:c1])
+            nc.scalar.copy(win[t][:, c0:c1], acc)
+
+        z_half(0)
+        for t in range(PACK):
+            b_tile(t)
+        z_half(1)
+        a_part(0, 0, W)
+        a_part(0, W, S)
+        for t in range(1, PACK):
+            a_part(t, 0, S)
+        z_w = zq[1][:].bitcast(F32)
+
+        g6 = [sb([P, S], F32, f"g6{t}")[:] for t in range(3)] + [z_w[:, :S]]
         rec = []
         for t in range(PACK):
-            nc.vector.tensor_copy(g6[t][:], aux[t][:].indirect(n6_t[:]))
+            nc.vector.tensor_copy(g6[t], aux[t][:].indirect(n6_t[:]))
         for t in range(PACK):
-            tr = bank(f"tr{t % 2}", f"den{t}")
+            tr = bank(("bk1","mm0","bk1","mm0")[t], f"den{t}")
             for blk in range(4):
                 cols = slice(P * blk, P * (blk + 1))
                 add_transposed(tr[:, cols], [aux[t][:, cols], g6[t][:, cols]])
             rs = sb([P, S], F32, f"rs{t}")
-            nc.scalar.activation(rs[:], tr[:], ACT.Abs_reciprocal_sqrt, bias=half[:])
+            nc.scalar.activation(rs[:], tr[:], ACT.Abs_reciprocal_sqrt, bias=half2[:])
             rq = sb([P, S], F32, f"rq{t}")
             nc.scalar.activation(rq[:], rs[:], ACT.Square)
-            rb = bank(f"mm{t}", f"rec{t}")
+            rb = bank(("mm2","mm3","bk0","tr1")[t], f"rec{t}")
             for blk in range(4):
                 cols = slice(P * blk, P * (blk + 1))
                 nc.tensor.transpose(rb[:, cols], rq[:, cols], ident[:])
             rec.append(rb)
 
         out_v = out.rearrange("(p t) c -> p t c", t=PACK)
-        g5 = [sb([P, S], F32, f"g5{t}") for t in range(PACK)]
-        num = [sb([P, S], F32, f"num{t}") for t in range(PACK)]
+        num = [sb([P, S], F32, f"num{t}")[:] for t in range(PACK)]
+        g5 = [sb([P, S], F32, f"g5{t}")[:] for t in range(3)] + num[:1]
         res = [sb([P, S], F32, f"res{t}") for t in range(PACK)]
-        for step in range(PACK + 2):
-            if step < PACK:
-                nc.vector.tensor_copy(g5[step][:], win[step][:].indirect(n5_t[:]))
-            if 1 <= step <= PACK:
-                t = step - 1
-                nc.vector.tensor_tensor(num[t][:], win[t][:, :S], g5[t][:], ALU.subtract)
-            if step >= 2:
-                t = step - 2
-                nc.vector.tensor_tensor(res[t][:], num[t][:], rec[t][:], ALU.mult)
-                nc.sync.dma_start(out_v[:, t, :], res[t][:])
+
+        def fetch(t):
+            nc.vector.tensor_copy(g5[t], win[t][:].indirect(n5_t[:]))
+
+        def diff(t, c0, c1):
+            nc.vector.tensor_tensor(num[t][:, c0:c1], win[t][:, c0:c1], g5[t][:, c0:c1], ALU.subtract)
+
+        def emit(t, c0, c1, queue):
+            nc.vector.tensor_tensor(res[t][:, c0:c1], num[t][:, c0:c1], rec[t][:, c0:c1], ALU.mult)
+            queue.dma_start(out_v[:, t, c0:c1], res[t][:, c0:c1])
+
+        fetch(0)
+        fetch(1)
+        diff(0, 0, S)
+        diff(1, 0, S)
+        fetch(2)
+        emit(0, 0, S, nc.sync)
+        fetch(3)
+        diff(2, 0, S)
+        emit(1, 0, S, nc.sync)
+        diff(3, 0, W)
+        emit(2, 0, S, nc.sync)
+        diff(3, W, S)
+        emit(3, 0, W, nc.sync)
+        emit(3, W, S, nc.scalar)

@@ -3,7 +3,7 @@ from contextlib import ExitStack
 import concourse.mybir as mybir
 from concourse.masks import make_identity
 
-K, T, S, H, W = 512, 2048, 512, 512, 256
+T, S, H, W = 2048, 512, 512, 256
 FLOPS = 3 * 2 * 512 * 512 * 512
 
 F32 = mybir.dt.float32
@@ -39,6 +39,14 @@ def tile_picked_tienormblapduel_none_p_kernel(
 
         def bank(tag, name):
             return psum.tile([P, 512], F32, name=name, tag=tag)
+
+        def half_of(lst, h):
+            return lst[:, 16 * h : 16 * (h + 1)]
+
+        def mx(acc, w_c, w_s, t, r_c, r_s):
+            cols = slice(P * t, P * (t + 1))
+            nc.tensor.matmul_mx(acc, lhsT=w_c[:, cols].bitcast(FP8X4), lhsT_scale=w_s[:, cols],
+                                rhs=r_c.bitcast(FP8X4), rhs_scale=r_s, start=True, stop=True)
 
         xs = sb([P, T], U8, "xs")
         nc.vector.memset(xs[:].bitcast(I32), 0)
@@ -97,30 +105,20 @@ def tile_picked_tienormblapduel_none_p_kernel(
         nc.vector.quantize_mx(w1_c[:].bitcast(FP8X4), w1_s[:], w1_bf[:])
         xg = sb([P, S], U32, "xg")
         for h in range(2):
-            nc.vector.tensor_copy(xg[:, W * h : W * (h + 1)], xw[:].bitcast(U32).indirect(offs_t[:, 16 * h : 16 * (h + 1)]))
-
-        def product(w_c, w_s, r_c, r_s, name):
-            banks = []
-            for t in range(PACK):
-                acc = bank(f"mm{t}", f"{name}{t}")
-                cols = slice(P * t, P * (t + 1))
-                nc.tensor.matmul_mx(acc[:], lhsT=w_c[:, cols].bitcast(FP8X4), lhsT_scale=w_s[:, cols],
-                                    rhs=r_c[:].bitcast(FP8X4), rhs_scale=r_s[:], start=True, stop=True)
-                banks.append(acc)
-            return banks
+            nc.vector.tensor_copy(xg[:, W * h : W * (h + 1)], xw[:].bitcast(U32).indirect(half_of(offs_t, h)))
 
         pieces = []
         for tag, t, c0, c1 in [("tr0", 0, 0, W), ("mm0", 0, W, S)] + [(f"mm{t}", t, 0, S) for t in range(1, PACK)]:
             acc = bank(tag, f"y{t}{c0}")[:, : c1 - c0]
-            cols = slice(P * t, P * (t + 1))
-            nc.tensor.matmul_mx(acc, lhsT=w1_c[:, cols].bitcast(FP8X4), lhsT_scale=w1_s[:, cols],
-                                rhs=xg[:, c0:c1].bitcast(FP8X4), rhs_scale=sg[:, c0:c1], start=True, stop=True)
+            mx(acc, w1_c, w1_s, t, xg[:, c0:c1], sg[:, c0:c1])
             pieces.append((acc, t, c0, c1))
         for i, (acc, t, c0, c1) in enumerate(pieces):
             if i == 1:
                 nc.vector.tensor_scalar(win[t][:, c0:c1], acc, gain[:, t : t + 1], None, ALU.mult)
             else:
                 nc.scalar.activation(win[t][:, c0:c1], acc, ACT.Copy, scale=gain[:, t : t + 1])
+        for acc, t, c0, c1 in pieces:
+            nc.scalar.activation(aux[t][:, S + c0 : S + c1], acc, ACT.Copy, scale=cgain[:, t : t + 1])
 
         pab2 = [sb([P, 2 * S], F32, f"pab{u}") for u in range(2)]
         pab = [pab2[t // 2][:, S * (t % 2) : S * (t % 2 + 1)] for t in range(PACK)]
@@ -131,12 +129,15 @@ def tile_picked_tienormblapduel_none_p_kernel(
         sbb = [x[:, W:] for x in sab]
         df = [sb([P, 2 * W], F32, f"df{u}") for u in range(2)]
         dt = [sb([P, S], F32, f"dt{t}") for t in range(PACK)]
-
-        def duel_fetch(t):
-            nc.vector.tensor_copy(pa[t], win[t][:].indirect(n3_t[:]))
-            nc.vector.tensor_copy(pb[t], win[t][:].indirect(n4_t[:]))
+        sums = [sb([P, PACK, W], F32, f"sums{h}") for h in range(2)]
+        zq = [sb([P, 2 * S], BF16, f"zq{h}") for h in range(2)]
+        z_c = sb([P, S], U32, "zc")
+        z_s = sb([P, S], U8, "zs")
 
         def duel_gate(u):
+            for t in (2 * u, 2 * u + 1):
+                nc.vector.tensor_copy(pa[t], win[t][:].indirect(n3_t[:]))
+                nc.vector.tensor_copy(pb[t], win[t][:].indirect(n4_t[:]))
             pv = pab2[u][:].rearrange("p (e s w) -> p e s w", e=2, s=2)
             nc.vector.tensor_tensor(df[u][:].rearrange("p (e w) -> p e w", e=2), pv[:, :, 1, :], pv[:, :, 0, :], ALU.subtract)
             for dst, scale in ((sa, ninv), (sbb, inv)):
@@ -144,68 +145,27 @@ def tile_picked_tienormblapduel_none_p_kernel(
                     t = 2 * u + e
                     nc.scalar.activation(dst[t], df[u][:, W * e : W * (e + 1)], ACT.Sigmoid, scale=scale[:, t : t + 1])
 
-        def put_a(t):
-            nc.vector.tensor_tensor(dt[t][:].indirect(n3_t[:]), pa[t], sa[t], ALU.mult)
-
-        def put_b(t):
-            nc.vector.tensor_tensor(dt[t][:].indirect(n4_t[:]), pb[t], sbb[t], ALU.mult)
-
-        def add_transposed(dst, terms):
-            for i, term in enumerate(terms):
-                nc.tensor.matmul(dst, lhsT=term, rhs=ident[:], is_transpose=True, start=(i == 0), stop=(i == len(terms) - 1))
-
-        def turn_pair(u, terms_of, scale, name, tags):
-            trs = [bank(tags[h], f"{name}tr{u}{h}") for h in range(2)]
+        def z_pair(h, u, room):
             for e in range(2):
-                terms = terms_of(2 * u + e)
-                for b in range(2):
-                    for i, term in enumerate(terms):
-                        for h in range(2):
-                            blk = 2 * h + b
-                            nc.tensor.matmul(trs[h][:, 2 * P * b + P * e : 2 * P * b + P * (e + 1)], lhsT=term[:, P * blk : P * (blk + 1)],
-                                             rhs=ident[:], is_transpose=True, start=(i == 0), stop=(i == len(terms) - 1))
-            res = []
-            for h in range(2):
-                zt = sb([P, 512], BF16, f"{name}zt{u}{h}")
-                nc.scalar.activation(zt[:].rearrange("p (b m e) -> p b m e", b=2, e=2),
-                                     trs[h][:].rearrange("p (b e m) -> p b m e", b=2, e=2), ACT.Copy, scale=scale)
-                res.append(zt)
-            return res
+                t = 2 * u + e
+                nc.vector.tensor_tensor(room[e], win[t][:].indirect(half_of(n1_t, h)), aux[t][:, S + W * h : S + W * (h + 1)], ALU.add)
+            for e in range(2):
+                t = 2 * u + e
+                nc.vector.tensor_tensor(sums[h][:, t, :], win[t][:].indirect(half_of(n2_t, h)), room[e], ALU.add)
 
-        def back_pair(u, zts, bks):
-            for h in range(2):
-                words = zts[h][:].bitcast(F32)
-                for b in range(2):
-                    nc.tensor.transpose(bks[h][:, 256 * u + P * b : 256 * u + P * (b + 1)], words[:, P * b : P * (b + 1)], ident[:])
+        def z_finish(h):
+            nc.scalar.activation(zq[h][:].rearrange("p (j t) -> p j t", t=PACK), sums[h][:].rearrange("p t j -> p j t"), ACT.Copy, scale=0.75)
+            nc.vector.quantize_mx(z_c[:, W * h : W * (h + 1)].bitcast(FP8X4), z_s[:, W * h : W * (h + 1)], zq[h][:])
 
-        def finish(bks, name):
-            zq = sb([P, PACK * S], BF16, f"{name}q")
-            zw = zq[:].bitcast(F32).rearrange("p (j u) -> p j u", u=2)
-            for h in range(2):
-                nc.scalar.copy(zw[:, 256 * h : 256 * (h + 1), :], bks[h][:].rearrange("p (u j) -> p j u", u=2))
-            codes = sb([P, S], U32, f"{name}c")
-            scales = sb([P, S], U8, f"{name}s")
-            nc.vector.quantize_mx(codes[:].bitcast(FP8X4), scales[:], zq[:])
-            return codes, scales, zq[:].bitcast(F32)
-
-        duel_fetch(0)
-        duel_fetch(1)
         duel_gate(0)
-        duel_fetch(2)
-        duel_fetch(3)
         duel_gate(1)
         half2 = sb([P, 1], F32, "half2")
         nc.scalar.activation(half2[:], sbb[3][:, 0:1], ACT.Abs_reciprocal_sqrt, bias=four[:], scale=0.0)
-        for acc, t, c0, c1 in pieces:
-            nc.scalar.activation(aux[t][:, S + c0 : S + c1], acc, ACT.Copy, scale=cgain[:, t : t + 1])
-        bks1 = [bank(f"mm{2 + h}", f"zbk{h}") for h in range(2)]
-        g1 = [sb([P, S], F32, "g10")[:], sb([P, S], F32, "g11")[:]]
-        g2 = [sb([P, S], F32, "g20")[:], sb([P, S], F32, "g21")[:]]
-        for t in range(2):
-            nc.vector.tensor_copy(g1[t], win[t][:].indirect(n1_t[:]))
-            nc.vector.tensor_copy(g2[t], win[t][:].indirect(n2_t[:]))
-        zts = turn_pair(0, lambda t: [aux[t][:, S:], g1[t], g2[t]], 0.75, "z", ("tr0", "tr1"))
-        back_pair(0, zts, bks1)
+        for u in range(2):
+            part = sb([P, S], F32, f"part{u}")
+            z_pair(0, u, [part[:, :W], part[:, W:]])
+        z_finish(0)
+
         w2_bf = sb([P, PACK * H], BF16, "w2_bf")
         w2_bv = w2_bf[:].rearrange("p (t m j) -> p m t j", t=PACK, j=PACK)
         w2_rv = w2_raw[:].rearrange("p j (m t) -> p m t j", t=PACK)
@@ -215,112 +175,98 @@ def tile_picked_tienormblapduel_none_p_kernel(
         w2_s = sb([P, H], U8, "w2_s")
         nc.vector.quantize_mx(w2_c[:].bitcast(FP8X4), w2_s[:], w2_bf[:])
 
-        bks2 = [bank(f"bk{h}", f"z2bk{h}") for h in range(2)]
+        back = [bank(f"bk{h}", f"z2bk{h}") for h in range(2)]
         for u in range(2):
-            put_a(2 * u)
-            put_a(2 * u + 1)
-            put_b(2 * u)
-            put_b(2 * u + 1)
-            zts = turn_pair(u, lambda t: [dt[t]], 1.0, "z2", ("tr0", "tr1"))
-            back_pair(u, zts, bks2)
+            for src, gate, lst in ((pa, sa, n3_t), (pb, sbb, n4_t)):
+                for t in (2 * u, 2 * u + 1):
+                    nc.vector.tensor_tensor(dt[t][:].indirect(lst[:]), src[t], gate[t], ALU.mult)
+            trs = [bank(f"tr{h}", f"z2tr{u}{h}") for h in range(2)]
+            for e in range(2):
+                for b in range(2):
+                    for h in range(2):
+                        blk = 2 * h + b
+                        nc.tensor.transpose(trs[h][:, 2 * P * b + P * e : 2 * P * b + P * (e + 1)], dt[2 * u + e][:, P * blk : P * (blk + 1)], ident[:])
+            for h in range(2):
+                zt = sb([P, 512], BF16, f"z2zt{u}{h}")
+                nc.scalar.copy(zt[:].rearrange("p (b m e) -> p b m e", b=2, e=2), trs[h][:].rearrange("p (b e m) -> p b m e", b=2, e=2))
+                words = zt[:].bitcast(F32)
+                for b in range(2):
+                    nc.tensor.transpose(back[h][:, W * u + P * b : W * u + P * (b + 1)], words[:, P * b : P * (b + 1)], ident[:])
+        z2q = sb([P, PACK * S], BF16, "z2q")
+        z2_w = z2q[:].bitcast(F32)
+        for h in range(2):
+            nc.scalar.copy(z2_w.rearrange("p (j u) -> p j u", u=2)[:, W * h : W * (h + 1), :], back[h][:].rearrange("p (u j) -> p j u", u=2))
+        z2_c = sb([P, S], U32, "z2c")
+        z2_s = sb([P, S], U8, "z2s")
+        nc.vector.quantize_mx(z2_c[:].bitcast(FP8X4), z2_s[:], z2q[:])
 
-        def mx(acc, w_c, w_s, t, r_c, r_s):
-            cols = slice(P * t, P * (t + 1))
-            nc.tensor.matmul_mx(acc, lhsT=w_c[:, cols].bitcast(FP8X4), lhsT_scale=w_s[:, cols],
-                                rhs=r_c.bitcast(FP8X4), rhs_scale=r_s, start=True, stop=True)
-
-        z2_c, z2_s, z2_w = finish(bks2, "z2")
+        neg = [sb([P, S], F32, f"neg{t}") for t in range(PACK)]
+        g6 = [sb([P, S], F32, f"g6{t}")[:] for t in range(PACK)]
+        g6[2] = zq[1][:].bitcast(F32)
+        rec = []
 
         def b_tile(t):
             acc = bank(("mm0", "mm1", "tr0", "tr1")[t], f"b{t}")
             mx(acc[:], w2_c, w2_s, t, z2_c[:], z2_s[:])
             nc.scalar.activation(aux[t][:, :S], acc[:], ACT.Abs)
 
-        room = [[pab[3][:, :W], pab[3][:, W:], sab[3][:, :W], sab[3][:, W:]], [z2_w[:, W * i : W * (i + 1)] for i in range(4)]]
-        zq = [sb([P, 2 * S], BF16, f"zq{h}") for h in range(2)]
-        z_c = sb([P, S], U32, "zc")
-        z_s = sb([P, S], U8, "zs")
-
-        def z_half(h):
-            trs = [bank(f"bk{blk}", f"ztr{h}{blk}") for blk in range(2)]
-            for e in range(2):
-                t = 2 + e
-                f1, f2 = room[h][2 * e], room[h][2 * e + 1]
-                nc.vector.tensor_copy(f1, win[t][:].indirect(n1_t[:, 16 * h : 16 * (h + 1)]))
-                nc.vector.tensor_copy(f2, win[t][:].indirect(n2_t[:, 16 * h : 16 * (h + 1)]))
-                terms = [aux[t][:, S + W * h : S + W * (h + 1)], f1, f2]
-                for i in range(3):
-                    for blk in range(2):
-                        nc.tensor.matmul(trs[blk][:, P * e : P * (e + 1)], lhsT=terms[i][:, P * blk : P * (blk + 1)], rhs=ident[:],
-                                         is_transpose=True, start=(i == 0), stop=(i == 2))
-            for blk in range(2):
-                zt = sb([P, W], BF16, f"zt1{h}{blk}")
-                nc.scalar.activation(zt[:].rearrange("p (m e) -> p m e", e=2),
-                                     trs[blk][:, :W].rearrange("p (e m) -> p m e", e=2), ACT.Copy, scale=0.75)
-                nc.tensor.transpose(bks1[h][:, W + P * blk : W + P * (blk + 1)], zt[:].bitcast(F32), ident[:])
-            nc.scalar.copy(zq[h][:].bitcast(F32).rearrange("p (j u) -> p j u", u=2), bks1[h][:].rearrange("p (u j) -> p j u", u=2))
-            nc.vector.quantize_mx(z_c[:, W * h : W * (h + 1)].bitcast(FP8X4), z_s[:, W * h : W * (h + 1)], zq[h][:])
-
-        def a_part(t, c0, c1):
-            acc = bank(("mm0", "mm1", "tr0", "tr1")[t], f"a{t}{c0}")[:, : c1 - c0]
+        def a_part(t, c0, c1, tag):
+            acc = bank(tag, f"a{t}{c0}")[:, : c1 - c0]
             mx(acc, w2_c, w2_s, t, z_c[:, c0:c1], z_s[:, c0:c1])
-            nc.scalar.copy(win[t][:, c0:c1], acc)
+            nc.scalar.mul(win[t][:, c0:c1], acc, -1.0)
+            nc.scalar.copy(neg[t][:, c0:c1], acc)
 
-        z_half(0)
-        for t in range(PACK):
-            b_tile(t)
-        z_half(1)
-        a_part(0, 0, W)
-        a_part(0, W, S)
-        for t in range(1, PACK):
-            a_part(t, 0, S)
-        z_w = zq[1][:].bitcast(F32)
-
-        g6 = [sb([P, S], F32, f"g6{t}")[:] for t in range(3)] + [z_w[:, :S]]
-        rec = []
-        for t in range(PACK):
+        def den_tile(t):
             nc.vector.tensor_copy(g6[t], aux[t][:].indirect(n6_t[:]))
-        for t in range(PACK):
-            tr = bank(("bk1","mm0","bk1","mm0")[t], f"den{t}")
+            tr = bank(("mm2","mm0","mm1","tr0")[t], f"den{t}")
             for blk in range(4):
                 cols = slice(P * blk, P * (blk + 1))
-                add_transposed(tr[:, cols], [aux[t][:, cols], g6[t][:, cols]])
+                for i, term in enumerate((aux[t][:, cols], g6[t][:, cols])):
+                    nc.tensor.matmul(tr[:, cols], lhsT=term, rhs=ident[:], is_transpose=True, start=(i == 0), stop=(i == 1))
             rs = sb([P, S], F32, f"rs{t}")
             nc.scalar.activation(rs[:], tr[:], ACT.Abs_reciprocal_sqrt, bias=half2[:])
             rq = sb([P, S], F32, f"rq{t}")
             nc.scalar.activation(rq[:], rs[:], ACT.Square)
-            rb = bank(("mm2","mm3","bk0","tr1")[t], f"rec{t}")
+            rb = bank(("mm3","bk0","bk1","mm2")[t], f"rec{t}")
             for blk in range(4):
                 cols = slice(P * blk, P * (blk + 1))
                 nc.tensor.transpose(rb[:, cols], rq[:, cols], ident[:])
             rec.append(rb)
 
+        z_pair(1, 0, [pab[3][:, W:], pab[3][:, :W]])
+        g6[3] = sums[1][:].rearrange("p t j -> p (t j)")[:, :S]
+        for t in range(PACK):
+            b_tile(t)
+        z_pair(1, 1, [z2_w[:, :W], z2_w[:, W : 2 * W]])
+        z_finish(1)
+        a_part(0, 0, W, "bk0")
+        a_part(1, 0, W, "bk1")
+        a_part(0, W, S, "mm0")
+        a_part(1, W, S, "mm1")
+        a_part(2, 0, S, "tr0")
+        a_part(3, 0, S, "tr1")
+        den_tile(0)
+        den_tile(1)
+        den_tile(2)
+        den_tile(3)
+
         out_v = out.rearrange("(p t) c -> p t c", t=PACK)
         num = [sb([P, S], F32, f"num{t}")[:] for t in range(PACK)]
-        g5 = [sb([P, S], F32, f"g5{t}")[:] for t in range(3)] + num[:1]
         res = [sb([P, S], F32, f"res{t}") for t in range(PACK)]
 
-        def fetch(t):
-            nc.vector.tensor_copy(g5[t], win[t][:].indirect(n5_t[:]))
-
-        def diff(t, c0, c1):
-            nc.vector.tensor_tensor(num[t][:, c0:c1], win[t][:, c0:c1], g5[t][:, c0:c1], ALU.subtract)
+        def diff(t):
+            nc.vector.tensor_tensor(num[t], win[t][:].indirect(n5_t[:]), neg[t][:], ALU.add)
 
         def emit(t, c0, c1, queue):
             nc.vector.tensor_tensor(res[t][:, c0:c1], num[t][:, c0:c1], rec[t][:, c0:c1], ALU.mult)
             queue.dma_start(out_v[:, t, c0:c1], res[t][:, c0:c1])
 
-        fetch(0)
-        fetch(1)
-        diff(0, 0, S)
-        diff(1, 0, S)
-        fetch(2)
+        diff(0)
+        diff(1)
+        diff(2)
         emit(0, 0, S, nc.sync)
-        fetch(3)
-        diff(2, 0, S)
+        diff(3)
         emit(1, 0, S, nc.sync)
-        diff(3, 0, W)
         emit(2, 0, S, nc.sync)
-        diff(3, W, S)
         emit(3, 0, W, nc.sync)
         emit(3, W, S, nc.scalar)

@@ -18,6 +18,7 @@ ACT = mybir.ActivationFunctionType
 
 P = 128
 PACK = 4
+FUSED = (3,)
 
 
 def tile_picked_tienormblapduel_none_p_kernel(
@@ -34,8 +35,8 @@ def tile_picked_tienormblapduel_none_p_kernel(
             nc.sync.dma_start(tile[:], ap)
             return tile
 
-        def sb(shape, dtype, name):
-            return keep.tile(shape, dtype, name=name, align_bytes=64)
+        def sb(shape, dtype, name, tag=None):
+            return keep.tile(shape, dtype, name=name, tag=tag or name, align_bytes=64)
 
         def bank(tag, name):
             return psum.tile([P, 512], F32, name=name, tag=tag)
@@ -51,8 +52,6 @@ def tile_picked_tienormblapduel_none_p_kernel(
         xs = sb([P, T], U8, "xs")
         nc.vector.memset(xs[:].bitcast(I32), 0)
         offs_t = load_list(offs, "offs_t")
-        gain = sb([P, PACK], F32, "gain")
-        nc.sync.dma_start(gain[:], gn.rearrange("(p t) o -> p (t o)", t=PACK))
         w1_raw = [sb([P, PACK, 256], F32, f"w1_raw{h}") for h in range(2)]
         w1_v = w1.rearrange("(p j) c -> p j c", j=PACK)
         nc.sync.dma_start(w1_raw[0][:], w1_v[:, :, :256])
@@ -61,6 +60,8 @@ def tile_picked_tienormblapduel_none_p_kernel(
         nc.sync.dma_start(w1_raw[1][:], w1_v[:, :, 256:])
         xw = sb([P, T], I32, "xw")
         nc.sync.dma_start(xw[:], x_words[0].rearrange("p n t -> p (n t)").bitcast(I32))
+        gain = sb([P, PACK], F32, "gain")
+        nc.sync.dma_start(gain[:], gn.rearrange("(p t) o -> p (t o)", t=PACK))
         n3_t = load_list(n3, "n3_t")
         n4_t = load_list(n4, "n4_t")
         n1_t = load_list(n1, "n1_t")
@@ -77,35 +78,37 @@ def tile_picked_tienormblapduel_none_p_kernel(
         half = sb([P, 1], F32, "half")
         nc.scalar.activation(half[:], zero[:], ACT.Sigmoid)
 
+        self_w = sb([P, 1], F32, "self_w")
+        nc.vector.tensor_scalar(self_w[:], half[:], -8.0 / 3.0, None, ALU.mult)
+
         ident = sb([P, P], F32, "ident")
         make_identity(nc, ident[:])
 
-        win = [sb([P, 2 * S], F32, f"win{t}") for t in range(PACK)]
+        win = [sb([P, S], F32, f"win{t}") for t in range(PACK)]
         aux = [sb([P, 2 * S], F32, f"aux{t}") for t in range(PACK)]
-        for t in range(PACK):
-            nc.vector.memset(win[t][:, S:], 0.0)
-
-        safe = sb([P, PACK], F32, "safe")
-        inv = sb([P, PACK], F32, "inv")
-        ninv = sb([P, PACK], F32, "ninv")
-        cgain = sb([P, PACK], F32, "cgain")
-        nc.vector.scalar_tensor_tensor(safe[:], gain[:], 0.0, gain[:], ALU.is_equal, ALU.add)
-        nc.vector.tensor_scalar(cgain[:], gain[:], half[:], -8.0 / 3.0, ALU.mult, ALU.mult)
-        nc.vector.reciprocal(inv[:], safe[:])
-        nc.vector.tensor_scalar(ninv[:], inv[:], -1.0, None, ALU.mult)
+        awin = [sb([P, 2 * S], F32, f"awin{t}") for t in range(PACK)]
 
         sg = sb([P, S], U8, "sg")
         nc.vector.tensor_copy(sg[:], xs[:].indirect(offs_t[:]))
         w1_bf = sb([P, PACK * H], BF16, "w1_bf")
         w1_bv = w1_bf[:].rearrange("p (t m j) -> p m t j", t=PACK, j=PACK)
-        for h in range(2):
-            nc.vector.tensor_copy(w1_bv[:, 64 * h : 64 * (h + 1)], w1_raw[h][:].rearrange("p j (m t) -> p m t j", t=PACK))
+        w1_rv = [x[:].rearrange("p j (m t) -> p m t j", t=PACK) for x in w1_raw]
+        nc.vector.tensor_copy(w1_bv[:, :64], w1_rv[0])
+        nc.scalar.copy(w1_bv[:, 64:], w1_rv[1])
         w1_c = sb([P, H], U32, "w1_c")
         w1_s = sb([P, H], U8, "w1_s")
         nc.vector.quantize_mx(w1_c[:].bitcast(FP8X4), w1_s[:], w1_bf[:])
         xg = sb([P, S], U32, "xg")
         for h in range(2):
             nc.vector.tensor_copy(xg[:, W * h : W * (h + 1)], xw[:].bitcast(U32).indirect(half_of(offs_t, h)))
+
+        safe = sb([P, 2 * PACK], F32, "safe")
+        zq = [sb([P, 2 * S], BF16, f"zq{h}") for h in range(2)]
+        inv = zq[0][:].bitcast(F32)[:, :PACK]
+        ninv = zq[0][:].bitcast(F32)[:, PACK : 2 * PACK]
+        nc.vector.scalar_tensor_tensor(safe[:, :PACK], gain[:], 0.0, gain[:], ALU.is_equal, ALU.add)
+        nc.vector.scalar_tensor_tensor(safe[:, PACK:], gain[:], 0.0, gain[:], ALU.is_equal, ALU.subtract)
+        nc.vector.reciprocal(zq[0][:].bitcast(F32)[:, : 2 * PACK], safe[:])
 
         pieces = []
         for tag, t, c0, c1 in [("tr0", 0, 0, W), ("mm0", 0, W, S)] + [(f"mm{t}", t, 0, S) for t in range(1, PACK)]:
@@ -117,56 +120,77 @@ def tile_picked_tienormblapduel_none_p_kernel(
                 nc.vector.tensor_scalar(win[t][:, c0:c1], acc, gain[:, t : t + 1], None, ALU.mult)
             else:
                 nc.scalar.activation(win[t][:, c0:c1], acc, ACT.Copy, scale=gain[:, t : t + 1])
-        for acc, t, c0, c1 in pieces:
-            nc.scalar.activation(aux[t][:, S + c0 : S + c1], acc, ACT.Copy, scale=cgain[:, t : t + 1])
 
         pab2 = [sb([P, 2 * S], F32, f"pab{u}") for u in range(2)]
-        pab = [pab2[t // 2][:, S * (t % 2) : S * (t % 2 + 1)] for t in range(PACK)]
-        sab = [sb([P, S], F32, f"sab{t}")[:] for t in range(PACK)]
-        pa = [x[:, :W] for x in pab]
-        pb = [x[:, W:] for x in pab]
+        sab = [aux[t][:, S:] for t in range(PACK)]
+        pa = [pab2[t // 2][:, W * (t % 2) : W * (t % 2 + 1)] for t in range(PACK)]
+        pb = [pab2[t // 2][:, S + W * (t % 2) : S + W * (t % 2 + 1)] for t in range(PACK)]
         sa = [x[:, :W] for x in sab]
         sbb = [x[:, W:] for x in sab]
         df = [sb([P, 2 * W], F32, f"df{u}") for u in range(2)]
-        dt = [sb([P, S], F32, f"dt{t}") for t in range(PACK)]
-        sums = [sb([P, PACK, W], F32, f"sums{h}") for h in range(2)]
-        zq = [sb([P, 2 * S], BF16, f"zq{h}") for h in range(2)]
+        late = sb([P, 3 * S], F32, "late")
+        sums = [sb([P, PACK * W], F32, "sums0")[:], late[:, : 2 * S]]
+        sums = [x.rearrange("p (t j) -> p t j", t=PACK) for x in sums]
         z_c = sb([P, S], U32, "zc")
         z_s = sb([P, S], U8, "zs")
 
+        npa = [sb([P, S], F32, f"npa{u}") for u in range(2)]
+        turned = []
+        gaps = []
+
+        def duel_fetch(t):
+            nc.vector.tensor_copy(pa[t], win[t][:].indirect(n3_t[:]))
+            nc.vector.tensor_copy(pb[t], win[t][:].indirect(n4_t[:]))
+
+        def own_term(t):
+            nc.scalar.activation(awin[t][:, S:], win[t][:], ACT.Copy, scale=self_w[:])
+
+        def duel_sum(u):
+            own_term(2 * u)
+            nc.scalar.mul(npa[u][:], pab2[u][:, :S], -1.0)
+            own_term(2 * u + 1)
+            turned.append(bank(("bk0", "tr1")[u], f"dT{u}"))
+            for blk in (0, 2, 1, 3):
+                cols = slice(P * blk, P * (blk + 1))
+                for i, term in enumerate((npa[u][:, cols], pab2[u][:, S:][:, cols])):
+                    nc.tensor.matmul(turned[u][:, cols], lhsT=term, rhs=ident[:], is_transpose=True, start=(i == 0), stop=(i == 1))
+
+        def duel_back(u):
+            nc.scalar.copy(df[u][:], turned[u][:])
+            gaps.append(bank(("bk1", "tr0")[u], f"d{u}"))
+            for blk in range(4):
+                cols = slice(P * blk, P * (blk + 1))
+                nc.tensor.transpose(gaps[u][:, cols], df[u][:, cols], ident[:])
+
         def duel_gate(u):
-            for t in (2 * u, 2 * u + 1):
-                nc.vector.tensor_copy(pa[t], win[t][:].indirect(n3_t[:]))
-                nc.vector.tensor_copy(pb[t], win[t][:].indirect(n4_t[:]))
-            pv = pab2[u][:].rearrange("p (e s w) -> p e s w", e=2, s=2)
-            nc.vector.tensor_tensor(df[u][:].rearrange("p (e w) -> p e w", e=2), pv[:, :, 1, :], pv[:, :, 0, :], ALU.subtract)
             for dst, scale in ((sa, ninv), (sbb, inv)):
                 for e in range(2):
                     t = 2 * u + e
-                    nc.scalar.activation(dst[t], df[u][:, W * e : W * (e + 1)], ACT.Sigmoid, scale=scale[:, t : t + 1])
+                    nc.scalar.activation(dst[t], gaps[u][:, W * e : W * (e + 1)], ACT.Sigmoid, scale=scale[:, t : t + 1])
 
         def z_pair(h, u, room):
             for e in range(2):
                 t = 2 * u + e
-                nc.vector.tensor_tensor(room[e], win[t][:].indirect(half_of(n1_t, h)), aux[t][:, S + W * h : S + W * (h + 1)], ALU.add)
+                nc.vector.tensor_tensor(room[e], win[t][:].indirect(half_of(n1_t, h)), awin[t][:, S + W * h : S + W * (h + 1)], ALU.add)
             for e in range(2):
                 t = 2 * u + e
                 nc.vector.tensor_tensor(sums[h][:, t, :], win[t][:].indirect(half_of(n2_t, h)), room[e], ALU.add)
 
         def z_finish(h):
-            nc.scalar.activation(zq[h][:].rearrange("p (j t) -> p j t", t=PACK), sums[h][:].rearrange("p t j -> p j t"), ACT.Copy, scale=0.75)
+            nc.scalar.activation(zq[h][:].rearrange("p (j t) -> p j t", t=PACK), sums[h].rearrange("p t j -> p j t"), ACT.Copy, scale=0.75)
             nc.vector.quantize_mx(z_c[:, W * h : W * (h + 1)].bitcast(FP8X4), z_s[:, W * h : W * (h + 1)], zq[h][:])
 
-        duel_gate(0)
-        duel_gate(1)
+        for t in range(PACK):
+            duel_fetch(t)
+        for step in (duel_sum, duel_back, duel_gate):
+            for u in range(2):
+                step(u)
         half2 = sb([P, 1], F32, "half2")
         nc.scalar.activation(half2[:], sbb[3][:, 0:1], ACT.Abs_reciprocal_sqrt, bias=four[:], scale=0.0)
         for u in range(2):
-            part = sb([P, S], F32, f"part{u}")
-            z_pair(0, u, [part[:, :W], part[:, W:]])
-        z_finish(0)
+            z_pair(0, u, [npa[u][:, W:], npa[u][:, :W]])
 
-        w2_bf = sb([P, PACK * H], BF16, "w2_bf")
+        w2_bf = sb([P, PACK * H], BF16, "w2_bf", "df1")
         w2_bv = w2_bf[:].rearrange("p (t m j) -> p m t j", t=PACK, j=PACK)
         w2_rv = w2_raw[:].rearrange("p j (m t) -> p m t j", t=PACK)
         for h in range(4):
@@ -174,7 +198,19 @@ def tile_picked_tienormblapduel_none_p_kernel(
         w2_c = sb([P, H], U32, "w2_c")
         w2_s = sb([P, H], U8, "w2_s")
         nc.vector.quantize_mx(w2_c[:].bitcast(FP8X4), w2_s[:], w2_bf[:])
+        z_finish(0)
 
+        dt = [sb([P, S], F32, f"dt{t}", ("dt0", "dt1", "sums0", "zq0")[t]) for t in range(PACK)]
+        neg = [sb([P, S], F32, f"neg{t}") for t in range(PACK)]
+
+        def a_part(t, c0, c1, tag):
+            acc = bank(tag, f"a{t}{c0}")[:, : c1 - c0]
+            mx(acc, w2_c, w2_s, t, z_c[:, c0:c1], z_s[:, c0:c1])
+            nc.scalar.mul(awin[t][:, c0:c1], acc, -1.0)
+            nc.scalar.copy(neg[t][:, c0:c1], acc)
+
+        for t in range(PACK):
+            a_part(t, 0, W, f"mm{t}")
         back = [bank(f"bk{h}", f"z2bk{h}") for h in range(2)]
         for u in range(2):
             for src, gate, lst in ((pa, sa, n3_t), (pb, sbb, n4_t)):
@@ -192,81 +228,84 @@ def tile_picked_tienormblapduel_none_p_kernel(
                 words = zt[:].bitcast(F32)
                 for b in range(2):
                     nc.tensor.transpose(back[h][:, W * u + P * b : W * u + P * (b + 1)], words[:, P * b : P * (b + 1)], ident[:])
-        z2q = sb([P, PACK * S], BF16, "z2q")
-        z2_w = z2q[:].bitcast(F32)
+        z2_w = [late[:, 2 * S :], late[:, S : 2 * S]]
         for h in range(2):
-            nc.scalar.copy(z2_w.rearrange("p (j u) -> p j u", u=2)[:, W * h : W * (h + 1), :], back[h][:].rearrange("p (u j) -> p j u", u=2))
+            nc.scalar.copy(z2_w[h].rearrange("p (j u) -> p j u", u=2), back[h][:].rearrange("p (u j) -> p j u", u=2))
         z2_c = sb([P, S], U32, "z2c")
         z2_s = sb([P, S], U8, "z2s")
-        nc.vector.quantize_mx(z2_c[:].bitcast(FP8X4), z2_s[:], z2q[:])
+        for h in range(2):
+            nc.vector.quantize_mx(z2_c[:, W * h : W * (h + 1)].bitcast(FP8X4), z2_s[:, W * h : W * (h + 1)], z2_w[h].bitcast(BF16))
 
-        neg = [sb([P, S], F32, f"neg{t}") for t in range(PACK)]
         g6 = [sb([P, S], F32, f"g6{t}")[:] for t in range(PACK)]
-        g6[2] = zq[1][:].bitcast(F32)
+        size = {t: sb([P, S], F32, f"size{t}") for t in FUSED}
         rec = []
 
-        def b_tile(t):
-            acc = bank(("mm0", "mm1", "tr0", "tr1")[t], f"b{t}")
-            mx(acc[:], w2_c, w2_s, t, z2_c[:], z2_s[:])
-            nc.scalar.activation(aux[t][:, :S], acc[:], ACT.Abs)
+        def b_part(t, c0, c1, tag):
+            acc = bank(tag, f"b{t}{c0}")[:, : c1 - c0]
+            mx(acc, w2_c, w2_s, t, z2_c[:, c0:c1], z2_s[:, c0:c1])
+            nc.scalar.activation(aux[t][:, c0:c1], acc, ACT.Abs)
+            if t in FUSED:
+                nc.scalar.activation(size[t][:, c0:c1], acc, ACT.Abs)
 
-        def a_part(t, c0, c1, tag):
-            acc = bank(tag, f"a{t}{c0}")[:, : c1 - c0]
-            mx(acc, w2_c, w2_s, t, z_c[:, c0:c1], z_s[:, c0:c1])
-            nc.scalar.mul(win[t][:, c0:c1], acc, -1.0)
-            nc.scalar.copy(neg[t][:, c0:c1], acc)
+        rs = [sb([P, S], F32, f"rs{t}") for t in range(PACK)]
 
-        def den_tile(t):
+        def den_root(t):
+            if t in FUSED:
+                nc.vector.tensor_tensor(g6[t], aux[t][:].indirect(n6_t[:]), size[t][:], ALU.add)
+                nc.scalar.activation(rs[t][:], g6[t], ACT.Abs_reciprocal_sqrt, bias=half2[:])
+                return
             nc.vector.tensor_copy(g6[t], aux[t][:].indirect(n6_t[:]))
-            tr = bank(("mm2","mm0","mm1","tr0")[t], f"den{t}")
+            tr = bank(("mm2", "mm0", "mm2", "mm1")[t], f"den{t}")
             for blk in range(4):
                 cols = slice(P * blk, P * (blk + 1))
                 for i, term in enumerate((aux[t][:, cols], g6[t][:, cols])):
                     nc.tensor.matmul(tr[:, cols], lhsT=term, rhs=ident[:], is_transpose=True, start=(i == 0), stop=(i == 1))
-            rs = sb([P, S], F32, f"rs{t}")
-            nc.scalar.activation(rs[:], tr[:], ACT.Abs_reciprocal_sqrt, bias=half2[:])
+            nc.scalar.activation(rs[t][:], tr[:], ACT.Abs_reciprocal_sqrt, bias=half2[:])
+
+        def den_square(t):
             rq = sb([P, S], F32, f"rq{t}")
-            nc.scalar.activation(rq[:], rs[:], ACT.Square)
-            rb = bank(("mm3","bk0","bk1","mm2")[t], f"rec{t}")
+            nc.scalar.activation(rq[:], rs[t][:], ACT.Square)
+            if t in FUSED:
+                rec.append(rq)
+                return
+            rb = bank(("mm3", "bk1", "bk0", "tr0")[t], f"rec{t}")
             for blk in range(4):
                 cols = slice(P * blk, P * (blk + 1))
                 nc.tensor.transpose(rb[:, cols], rq[:, cols], ident[:])
             rec.append(rb)
 
-        z_pair(1, 0, [pab[3][:, W:], pab[3][:, :W]])
-        g6[3] = sums[1][:].rearrange("p t j -> p (t j)")[:, :S]
-        for t in range(PACK):
-            b_tile(t)
-        z_pair(1, 1, [z2_w[:, :W], z2_w[:, W : 2 * W]])
+        z_pair(1, 0, [pb[3], pa[3]])
+        z_pair(1, 1, [sbb[3], sa[3]])
+        b_part(0, 0, W, "mm2")
+        b_part(0, W, S, "mm0")
+        b_part(1, 0, S, "mm1")
         z_finish(1)
-        a_part(0, 0, W, "bk0")
-        a_part(1, 0, W, "bk1")
+        b_part(2, 0, S, "tr0")
+        b_part(3, 0, S, "tr1")
+        den_root(0)
         a_part(0, W, S, "mm0")
         a_part(1, W, S, "mm1")
-        a_part(2, 0, S, "tr0")
-        a_part(3, 0, S, "tr1")
-        den_tile(0)
-        den_tile(1)
-        den_tile(2)
-        den_tile(3)
+        a_part(2, W, S, "tr0")
+        a_part(3, W, S, "tr1")
+        for t in range(1, PACK):
+            den_root(t)
+            den_square(t - 1)
+        den_square(PACK - 1)
 
         out_v = out.rearrange("(p t) c -> p t c", t=PACK)
         num = [sb([P, S], F32, f"num{t}")[:] for t in range(PACK)]
         res = [sb([P, S], F32, f"res{t}") for t in range(PACK)]
 
-        def diff(t):
-            nc.vector.tensor_tensor(num[t], win[t][:].indirect(n5_t[:]), neg[t][:], ALU.add)
+        def diff(t, c0, c1):
+            nc.vector.tensor_tensor(num[t][:, c0:c1], awin[t][:].indirect(n5_t[:, c0 // 16 : c1 // 16]), neg[t][:, c0:c1], ALU.add)
 
         def emit(t, c0, c1, queue):
             nc.vector.tensor_tensor(res[t][:, c0:c1], num[t][:, c0:c1], rec[t][:, c0:c1], ALU.mult)
             queue.dma_start(out_v[:, t, c0:c1], res[t][:, c0:c1])
 
-        diff(0)
-        diff(1)
-        diff(2)
-        emit(0, 0, S, nc.sync)
-        diff(3)
-        emit(1, 0, S, nc.sync)
-        emit(2, 0, S, nc.sync)
+        for t in range(PACK):
+            diff(t, 0, S)
+        for t in range(PACK - 1):
+            emit(t, 0, S, nc.sync)
         emit(3, 0, W, nc.sync)
         emit(3, W, S, nc.scalar)

from contextlib import ExitStack

import concourse.mybir as mybir
from concourse.masks import make_identity

T, S, H, W = 2048, 512, 512, 256
FLOPS = 3 * 2 * 512 * 512 * 512

F32 = mybir.dt.float32
BF16 = mybir.dt.bfloat16
I32 = mybir.dt.int32
U32 = mybir.dt.uint32
U16 = mybir.dt.uint16
U8 = mybir.dt.uint8
FP8X4 = mybir.dt.float8_e4m3fn_x4
ALU = mybir.AluOpType
ACT = mybir.ActivationFunctionType

P = 128
PACK = 4
FUSED = (3,)


def tile_picked_tienormblapduel_none_p_kernel(
    tc, x_words, x_scales, w1, gn, w2, offs, n1, n2, n3, n4, n5, n6, out
):
    nc = tc.nc
    with ExitStack() as ctx:
        lists = ctx.enter_context(tc.tile_pool(name="lists", bufs=1))
        keep = ctx.enter_context(tc.tile_pool(name="keep", bufs=1))
        psum = ctx.enter_context(tc.psum_pool(name="psum", bufs=1))

        def load_list(ap, name):
            tile = lists.tile(list(ap.shape), U16, name=name)
            nc.sync.dma_start(tile[:], ap)
            return tile

        def sb(shape, dtype, name, tag=None):
            return keep.tile(shape, dtype, name=name, tag=tag or name, align_bytes=64)

        def bank(tag, name):
            return psum.tile([P, 512], F32, name=name, tag=tag)

        def half_of(lst, h):
            return lst[:, 16 * h : 16 * (h + 1)]

        def mx(acc, w_c, w_s, t, r_c, r_s):
            cols = slice(P * t, P * (t + 1))
            nc.tensor.matmul_mx(acc, lhsT=w_c[:, cols].bitcast(FP8X4), lhsT_scale=w_s[:, cols],
                                rhs=r_c.bitcast(FP8X4), rhs_scale=r_s, start=True, stop=True)

        xs = sb([P, T], U8, "xs")
        nc.vector.memset(xs[:].bitcast(I32), 0)
        offs_t = load_list(offs, "offs_t")
        w1_raw = [sb([P, PACK, 256], F32, f"w1_raw{h}") for h in range(2)]
        w1_v = w1.rearrange("(p j) c -> p j c", j=PACK)
        nc.sync.dma_start(w1_raw[0][:], w1_v[:, :, :256])
        for q in range(4):
            nc.sync.dma_start(xs[32 * q : 32 * q + 4, :].bitcast(I32), x_scales[0, 4 * q : 4 * q + 4, :].bitcast(I32))
        nc.sync.dma_start(w1_raw[1][:], w1_v[:, :, 256:])
        xw = sb([P, T], I32, "xw")
        nc.sync.dma_start(xw[:], x_words[0].rearrange("p n t -> p (n t)").bitcast(I32))
        gain = sb([P, PACK], F32, "gain")
        nc.sync.dma_start(gain[:], gn.rearrange("(p t) o -> p (t o)", t=PACK))
        n3_t = load_list(n3, "n3_t")
        n4_t = load_list(n4, "n4_t")
        n1_t = load_list(n1, "n1_t")
        n2_t = load_list(n2, "n2_t")
        n6_t = load_list(n6, "n6_t")
        n5_t = load_list(n5, "n5_t")
        w2_raw = sb([P, PACK, H], F32, "w2_raw")
        nc.sync.dma_start(w2_raw[:], w2.rearrange("(p j) c -> p j c", j=PACK))

        zero = sb([P, 1], F32, "zero")
        nc.vector.memset(zero[:], 0.0)
        four = sb([P, 1], F32, "four")
        nc.vector.memset(four[:], 4.0)
        half = sb([P, 1], F32, "half")
        nc.scalar.activation(half[:], zero[:], ACT.Sigmoid)

        self_w = sb([P, 1], F32, "self_w")
        nc.vector.tensor_scalar(self_w[:], half[:], -8.0 / 3.0, None, ALU.mult)

        ident = sb([P, P], F32, "ident")
        make_identity(nc, ident[:])

        win = [sb([P, S], F32, f"win{t}") for t in range(PACK)]
        aux = [sb([P, 2 * S], F32, f"aux{t}") for t in range(PACK)]
        awin = [sb([P, 2 * S], F32, f"awin{t}") for t in range(PACK)]

        sg = sb([P, S], U8, "sg")
        nc.vector.tensor_copy(sg[:], xs[:].indirect(offs_t[:]))
        w1_bf = sb([P, PACK * H], BF16, "w1_bf")
        w1_bv = w1_bf[:].rearrange("p (t m j) -> p m t j", t=PACK, j=PACK)
        w1_rv = [x[:].rearrange("p j (m t) -> p m t j", t=PACK) for x in w1_raw]
        nc.vector.tensor_copy(w1_bv[:, :64], w1_rv[0])
        nc.scalar.copy(w1_bv[:, 64:], w1_rv[1])
        w1_c = sb([P, H], U32, "w1_c")
        w1_s = sb([P, H], U8, "w1_s")
        nc.vector.quantize_mx(w1_c[:].bitcast(FP8X4), w1_s[:], w1_bf[:])
        xg = sb([P, S], U32, "xg")
        for h in range(2):
            nc.vector.tensor_copy(xg[:, W * h : W * (h + 1)], xw[:].bitcast(U32).indirect(half_of(offs_t, h)))

        safe = sb([P, 2 * PACK], F32, "safe")
        zq = [sb([P, 2 * S], BF16, f"zq{h}") for h in range(2)]
        inv = zq[0][:].bitcast(F32)[:, :PACK]
        ninv = zq[0][:].bitcast(F32)[:, PACK : 2 * PACK]
        nc.vector.scalar_tensor_tensor(safe[:, :PACK], gain[:], 0.0, gain[:], ALU.is_equal, ALU.add)
        nc.vector.scalar_tensor_tensor(safe[:, PACK:], gain[:], 0.0, gain[:], ALU.is_equal, ALU.subtract)
        nc.vector.reciprocal(zq[0][:].bitcast(F32)[:, : 2 * PACK], safe[:])

        pieces = []
        for tag, t, c0, c1 in [("tr0", 0, 0, W), ("mm0", 0, W, S)] + [(f"mm{t}", t, 0, S) for t in range(1, PACK)]:
            acc = bank(tag, f"y{t}{c0}")[:, : c1 - c0]
            mx(acc, w1_c, w1_s, t, xg[:, c0:c1], sg[:, c0:c1])
            pieces.append((acc, t, c0, c1))
        for i, (acc, t, c0, c1) in enumerate(pieces):
            if i == 1:
                nc.vector.tensor_scalar(win[t][:, c0:c1], acc, gain[:, t : t + 1], None, ALU.mult)
            else:
                nc.scalar.activation(win[t][:, c0:c1], acc, ACT.Copy, scale=gain[:, t : t + 1])

        pab2 = [sb([P, 2 * S], F32, f"pab{u}") for u in range(2)]
        sab = [aux[t][:, S:] for t in range(PACK)]
        pa = [pab2[t // 2][:, W * (t % 2) : W * (t % 2 + 1)] for t in range(PACK)]
        pb = [pab2[t // 2][:, S + W * (t % 2) : S + W * (t % 2 + 1)] for t in range(PACK)]
        sa = [x[:, :W] for x in sab]
        sbb = [x[:, W:] for x in sab]
        df = [sb([P, 2 * W], F32, f"df{u}") for u in range(2)]
        late = sb([P, 3 * S], F32, "late")
        sums = [sb([P, PACK * W], F32, "sums0")[:], late[:, : 2 * S]]
        sums = [x.rearrange("p (t j) -> p t j", t=PACK) for x in sums]
        z_c = sb([P, S], U32, "zc")
        z_s = sb([P, S], U8, "zs")

        npa = [sb([P, S], F32, f"npa{u}") for u in range(2)]
        turned = []
        gaps = []

        def duel_fetch(t):
            nc.vector.tensor_copy(pa[t], win[t][:].indirect(n3_t[:]))
            nc.vector.tensor_copy(pb[t], win[t][:].indirect(n4_t[:]))

        def own_term(t):
            nc.scalar.activation(awin[t][:, S:], win[t][:], ACT.Copy, scale=self_w[:])

        def duel_sum(u):
            own_term(2 * u)
            nc.scalar.mul(npa[u][:], pab2[u][:, :S], -1.0)
            own_term(2 * u + 1)
            turned.append(bank(("bk0", "tr1")[u], f"dT{u}"))
            for blk in (0, 2, 1, 3):
                cols = slice(P * blk, P * (blk + 1))
                for i, term in enumerate((npa[u][:, cols], pab2[u][:, S:][:, cols])):
                    nc.tensor.matmul(turned[u][:, cols], lhsT=term, rhs=ident[:], is_transpose=True, start=(i == 0), stop=(i == 1))

        def duel_back(u):
            nc.scalar.copy(df[u][:], turned[u][:])
            gaps.append(bank(("bk1", "tr0")[u], f"d{u}"))
            for blk in range(4):
                cols = slice(P * blk, P * (blk + 1))
                nc.tensor.transpose(gaps[u][:, cols], df[u][:, cols], ident[:])

        def duel_gate(u):
            for dst, scale in ((sa, ninv), (sbb, inv)):
                for e in range(2):
                    t = 2 * u + e
                    nc.scalar.activation(dst[t], gaps[u][:, W * e : W * (e + 1)], ACT.Sigmoid, scale=scale[:, t : t + 1])

        def z_pair(h, u, room):
            for e in range(2):
                t = 2 * u + e
                nc.vector.tensor_tensor(room[e], win[t][:].indirect(half_of(n1_t, h)), awin[t][:, S + W * h : S + W * (h + 1)], ALU.add)
            for e in range(2):
                t = 2 * u + e
                nc.vector.tensor_tensor(sums[h][:, t, :], win[t][:].indirect(half_of(n2_t, h)), room[e], ALU.add)

        def z_finish(h):
            nc.scalar.activation(zq[h][:].rearrange("p (j t) -> p j t", t=PACK), sums[h].rearrange("p t j -> p j t"), ACT.Copy, scale=0.75)
            nc.vector.quantize_mx(z_c[:, W * h : W * (h + 1)].bitcast(FP8X4), z_s[:, W * h : W * (h + 1)], zq[h][:])

        for t in range(PACK):
            duel_fetch(t)
        for step in (duel_sum, duel_back, duel_gate):
            for u in range(2):
                step(u)
        half2 = sb([P, 1], F32, "half2")
        nc.scalar.activation(half2[:], sbb[3][:, 0:1], ACT.Abs_reciprocal_sqrt, bias=four[:], scale=0.0)
        for u in range(2):
            z_pair(0, u, [npa[u][:, W:], npa[u][:, :W]])

        w2_bf = sb([P, PACK * H], BF16, "w2_bf", "df1")
        w2_bv = w2_bf[:].rearrange("p (t m j) -> p m t j", t=PACK, j=PACK)
        w2_rv = w2_raw[:].rearrange("p j (m t) -> p m t j", t=PACK)
        for h in range(4):
            nc.scalar.copy(w2_bv[:, 32 * h : 32 * (h + 1)], w2_rv[:, 32 * h : 32 * (h + 1)])
        w2_c = sb([P, H], U32, "w2_c")
        w2_s = sb([P, H], U8, "w2_s")
        nc.vector.quantize_mx(w2_c[:].bitcast(FP8X4), w2_s[:], w2_bf[:])
        z_finish(0)

        dt = [sb([P, S], F32, f"dt{t}", ("dt0", "dt1", "sums0", "zq0")[t]) for t in range(PACK)]
        neg = [sb([P, S], F32, f"neg{t}") for t in range(PACK)]

        def a_part(t, c0, c1, tag):
            acc = bank(tag, f"a{t}{c0}")[:, : c1 - c0]
            mx(acc, w2_c, w2_s, t, z_c[:, c0:c1], z_s[:, c0:c1])
            nc.scalar.mul(awin[t][:, c0:c1], acc, -1.0)
            nc.scalar.copy(neg[t][:, c0:c1], acc)

        for t in range(PACK):
            a_part(t, 0, W, f"mm{t}")
        back = [bank(f"bk{h}", f"z2bk{h}") for h in range(2)]
        for u in range(2):
            for src, gate, lst in ((pa, sa, n3_t), (pb, sbb, n4_t)):
                for t in (2 * u, 2 * u + 1):
                    nc.vector.tensor_tensor(dt[t][:].indirect(lst[:]), src[t], gate[t], ALU.mult)
            trs = [bank(f"tr{h}", f"z2tr{u}{h}") for h in range(2)]
            for e in range(2):
                for b in range(2):
                    for h in range(2):
                        blk = 2 * h + b
                        nc.tensor.transpose(trs[h][:, 2 * P * b + P * e : 2 * P * b + P * (e + 1)], dt[2 * u + e][:, P * blk : P * (blk + 1)], ident[:])
            for h in range(2):
                zt = sb([P, 512], BF16, f"z2zt{u}{h}")
                nc.scalar.copy(zt[:].rearrange("p (b m e) -> p b m e", b=2, e=2), trs[h][:].rearrange("p (b e m) -> p b m e", b=2, e=2))
                words = zt[:].bitcast(F32)
                for b in range(2):
                    nc.tensor.transpose(back[h][:, W * u + P * b : W * u + P * (b + 1)], words[:, P * b : P * (b + 1)], ident[:])
        z2_w = [late[:, 2 * S :], late[:, S : 2 * S]]
        for h in range(2):
            nc.scalar.copy(z2_w[h].rearrange("p (j u) -> p j u", u=2), back[h][:].rearrange("p (u j) -> p j u", u=2))
        z2_c = sb([P, S], U32, "z2c")
        z2_s = sb([P, S], U8, "z2s")
        for h in range(2):
            nc.vector.quantize_mx(z2_c[:, W * h : W * (h + 1)].bitcast(FP8X4), z2_s[:, W * h : W * (h + 1)], z2_w[h].bitcast(BF16))

        g6 = [sb([P, S], F32, f"g6{t}")[:] for t in range(PACK)]
        size = {t: sb([P, S], F32, f"size{t}") for t in FUSED}
        rec = []

        def b_part(t, c0, c1, tag):
            acc = bank(tag, f"b{t}{c0}")[:, : c1 - c0]
            mx(acc, w2_c, w2_s, t, z2_c[:, c0:c1], z2_s[:, c0:c1])
            nc.scalar.activation(aux[t][:, c0:c1], acc, ACT.Abs)
            if t in FUSED:
                nc.scalar.activation(size[t][:, c0:c1], acc, ACT.Abs)

        rs = [sb([P, S], F32, f"rs{t}") for t in range(PACK)]

        def den_root(t):
            if t in FUSED:
                nc.vector.tensor_tensor(g6[t], aux[t][:].indirect(n6_t[:]), size[t][:], ALU.add)
                nc.scalar.activation(rs[t][:], g6[t], ACT.Abs_reciprocal_sqrt, bias=half2[:])
                return
            nc.vector.tensor_copy(g6[t], aux[t][:].indirect(n6_t[:]))
            tr = bank(("mm2", "mm0", "mm2", "mm1")[t], f"den{t}")
            for blk in range(4):
                cols = slice(P * blk, P * (blk + 1))
                for i, term in enumerate((aux[t][:, cols], g6[t][:, cols])):
                    nc.tensor.matmul(tr[:, cols], lhsT=term, rhs=ident[:], is_transpose=True, start=(i == 0), stop=(i == 1))
            nc.scalar.activation(rs[t][:], tr[:], ACT.Abs_reciprocal_sqrt, bias=half2[:])

        def den_square(t):
            rq = sb([P, S], F32, f"rq{t}")
            nc.scalar.activation(rq[:], rs[t][:], ACT.Square)
            if t in FUSED:
                rec.append(rq)
                return
            rb = bank(("mm3", "bk1", "bk0", "tr0")[t], f"rec{t}")
            for blk in range(4):
                cols = slice(P * blk, P * (blk + 1))
                nc.tensor.transpose(rb[:, cols], rq[:, cols], ident[:])
            rec.append(rb)

        z_pair(1, 0, [pb[3], pa[3]])
        z_pair(1, 1, [sbb[3], sa[3]])
        b_part(0, 0, W, "mm2")
        b_part(0, W, S, "mm0")
        b_part(1, 0, S, "mm1")
        z_finish(1)
        b_part(2, 0, S, "tr0")
        b_part(3, 0, S, "tr1")
        den_root(0)
        a_part(0, W, S, "mm0")
        a_part(1, W, S, "mm1")
        a_part(2, W, S, "tr0")
        a_part(3, W, S, "tr1")
        for t in range(1, PACK):
            den_root(t)
            den_square(t - 1)
        den_square(PACK - 1)

        out_v = out.rearrange("(p t) c -> p t c", t=PACK)
        num = [sb([P, S], F32, f"num{t}")[:] for t in range(PACK)]
        res = [sb([P, S], F32, f"res{t}") for t in range(PACK)]

        def diff(t, c0, c1):
            nc.vector.tensor_tensor(num[t][:, c0:c1], awin[t][:].indirect(n5_t[:, c0 // 16 : c1 // 16]), neg[t][:, c0:c1], ALU.add)

        def emit(t, c0, c1, queue):
            nc.vector.tensor_tensor(res[t][:, c0:c1], num[t][:, c0:c1], rec[t][:, c0:c1], ALU.mult)
            queue.dma_start(out_v[:, t, c0:c1], res[t][:, c0:c1])

        for t in range(PACK):
            diff(t, 0, S)
        for t in range(PACK - 1):
            emit(t, 0, S, nc.sync)
        emit(3, 0, W, nc.sync)
        emit(3, W, S, nc.scalar)
